import numpy as np, ml_dtypes
CORES = [0,1,2,3]
N = 4
ROOT = 2
def setup_inputs(rng):
    return {"x": rng.standard_normal((N, 128, N * 4), dtype=np.float32).astype(ml_dtypes.bfloat16)}
def reference(x):
    return {"y": np.stack([x[ROOT][:, r * 4:(r + 1) * 4] for r in range(N)])}

from concourse.bass import DstId, RemoteDMATransfer

SCRATCH = {
    "stage": ("dram", [4, 128, 4], "bfloat16"),
    "land": ("dram", [128, 4], "bfloat16"),
}
SEMAPHORES = ["packed_g", "packed_h", "sent", "arrived", "stored"]

W = 4
ENGINES = 4


def rank_program(g, core, T, topo):
    rank = T.rank_of(core)
    if rank is None:
        return
    root = 2 if T.root is None else T.root

    if rank != root:
        g.sync.wait_ge(T.sem.arrived, ENGINES)
        g.sync.dma_start(T.y[:], T.land[:]).then_inc(T.sem.stored, 16)
        g.sync.wait_ge(T.sem.stored, 16)
        return

    others = [r for r in range(len(T.cores)) if r != root]

    r0, r1, r2 = others
    g.sync.dma_start(T.stage[r0], T.x[:, r0 * W:(r0 + 1) * W]).then_inc(T.sem.packed_h, 16)
    g.scalar.dma_start(T.stage[r1], T.x[:, r1 * W:(r1 + 1) * W]).then_inc(T.sem.packed_h, 16)
    g.dma_start(T.stage[r2], T.x[:, r2 * W:(r2 + 1) * W]).then_inc(T.sem.packed_g, 16)
    g.sync.dma_start(T.y[:], T.x[:, root * W:(root + 1) * W]).then_inc(T.sem.stored, 16)

    g.wait_ge(T.sem.packed_g, 16)
    g.wait_ge(T.sem.packed_h, 32)
    transfers = []
    for k, r in enumerate(others):
        rid, pid, _se = topo.addr(T.cores[r])
        transfers.append(RemoteDMATransfer(
            dst_ids=[DstId(rid=rid, pnc=pid)],
            dma_engine_mask=((1 << ENGINES) - 1) << (k * ENGINES),
            remote_sem=T.sem.arrived,
            src=T.stage[r],
            dst=T.land[:],
        ))
    g.remote_dma_fused(transfers, local_sem=T.sem.sent)

    g.wait_ge(T.sem.sent, ENGINES * len(others))
    g.sync.wait_ge(T.sem.stored, 16)
